import numpy as np
import ml_dtypes


def mxq(x, axis, fmt="e4m3"):
    dtype, down = {"e4m3": (ml_dtypes.float8_e4m3fn, 7), "e5m2": (ml_dtypes.float8_e5m2, 14)}[fmt]
    v = np.moveaxis(np.asarray(x, np.float32).astype(ml_dtypes.bfloat16).astype(np.float64), axis, -1)
    blocks = v.reshape(v.shape[:-1] + (-1, 32))
    amax = np.abs(blocks).max(-1, keepdims=True)
    byte = np.maximum(np.where(amax > 0, np.frexp(amax)[1] - 1 + 127, 0) - down, 1)
    scale = np.exp2(byte - 127.0)
    codes = (blocks / scale).astype(np.float32).astype(dtype).astype(np.float64)
    return np.moveaxis((codes * scale).reshape(v.shape), -1, axis)


WIDE = False


def mx_kscale(k):
    if not WIDE:
        return np.ones(k)
    levels = np.array([10, -10, 5, -5, 0])
    if k % 512:
        return np.exp2(np.random.permutation(np.resize(levels, k // 32))).repeat(32)
    a = np.empty((k // 512, 16))
    for p in range(k // 512):
        a[p, :8] = np.random.permutation(np.resize(levels, 8))
        for g in range(8):
            far = levels[np.abs(levels - a[p, g]) >= 10]
            a[p, g + 8] = far[np.random.randint(len(far))]
    return np.exp2(a.ravel()).repeat(32)


def f64(x):
    return np.asarray(x).astype(np.float64)


E2M1 = np.array([0.0, 0.5, 1.0, 1.5, 2.0, 3.0, 4.0, 6.0, -0.0, -0.5, -1.0, -1.5, -2.0, -3.0, -4.0, -6.0])


def pack_weight(w, fmt):
    k, n = w.shape
    w = f64(np.asarray(w, np.float32).astype(ml_dtypes.bfloat16)).reshape(k // 32, 32, n)
    amax = np.abs(w).max(1)
    if fmt == "e4m3":
        byte = np.frexp(amax)[1] - 1 + 127 - 7
    else:
        mant, ex = np.frexp(amax / 6.0)
        byte = np.where(mant > 0.5, ex, ex - 1) + 127
    byte = np.clip(np.where(amax > 0, byte, 1), 1, 254)
    scaled = (w * np.exp2(127.0 - byte)[:, None, :]).reshape(k, n).astype(np.float32)
    by_word = np.ascontiguousarray(scaled.reshape(k // 512, 128, 4, n).transpose(0, 1, 3, 2))
    if fmt == "e4m3":
        words = by_word.astype(ml_dtypes.float8_e4m3fn).view(np.uint8)
    else:
        c = by_word.astype(ml_dtypes.float4_e2m1fn).view(np.uint8) & 0xF
        words = (c[..., 0::2] | (c[..., 1::2] << 4)).reshape(k // 512, 128, 2 * n)
    return np.ascontiguousarray(words), np.ascontiguousarray(byte.astype(np.uint8).reshape(k // 512, 16, n))


def unpack_weight(words, scales, fmt):
    g, _, n = scales.shape
    words = np.ascontiguousarray(words).reshape(g, 128, n, -1)
    if fmt == "e4m3":
        vals = words.view(ml_dtypes.float8_e4m3fn).astype(np.float64)
    else:
        nib = np.empty((g, 128, n, 4), np.uint8)
        nib[..., 0::2] = words & 0xF
        nib[..., 1::2] = words >> 4
        vals = E2M1[nib]
    vals = vals * np.repeat(np.exp2(scales.astype(np.float64) - 127.0), 8, axis=1)[..., None]
    return vals.transpose(0, 1, 3, 2).reshape(g * 512, n)


def planes(y):
    n, m = y.shape
    v = y.astype(np.float32).astype(ml_dtypes.bfloat16).astype(np.float64).reshape(n // 32, 32, m)
    top = np.abs(v).max(1)
    byte = np.clip(np.where(top > 0, np.frexp(top)[1] - 1 + 127 - 7, 1), 1, 254)
    codes = (v * np.exp2(127.0 - byte)[:, None, :]).reshape(n, m).astype(np.float32).astype(ml_dtypes.float8_e4m3fn).view(np.uint8)
    words = codes.reshape(n // 512, 128, 4, m).transpose(0, 1, 3, 2)
    return np.ascontiguousarray(words), np.ascontiguousarray(byte.astype(np.uint8).reshape(n // 512, 16, m))


def gelu(v):
    return 0.5 * v * (1.0 + np.tanh(np.sqrt(2.0 / np.pi) * (v + 0.044715 * v**3)))


O, K, M, T = 1024, 3072, 1536, 512


def setup_inputs():
    n = np.random.standard_normal
    s = mx_kscale(K)[:, None]
    x = n((K, T)); x[:O] *= 6.0
    w = n((K, M)) / np.sqrt(K) / s; w[:O] /= 2.0
    p_w8 = pack_weight(w[:O], "e4m3")
    p_w4 = pack_weight(w[O:], "e2m1")
    return {
        "x": (x * s).astype(np.float32),
        "w8_words": p_w8[0],
        "w8_scales": p_w8[1],
        "w4_words": p_w4[0],
        "w4_scales": p_w4[1],
        "b": (0.3 * n(1536)).astype(np.float32),
    }


def reference(x, w8_words, w8_scales, w4_words, w4_scales, b):
    x_ = mxq(f64(x), 0, "e4m3")
    w8_ = unpack_weight(w8_words, w8_scales, "e4m3")
    w4_ = unpack_weight(w4_words, w4_scales, "e2m1")
    y = w8_.T @ x_[:O] + w4_.T @ x_[O:]
    out_0 = gelu(y + f64(b)[:, None])
    return (out_0,) + planes(out_0)

@@ -1,0 +1,254 @@
+from contextlib import ExitStack
+
+import concourse.mybir as mybir
+
+O, K, M, T = 1024, 3072, 1536, 512
+FLOPS = 2 * K * M * T
+
+F32 = mybir.dt.float32
+BF16 = mybir.dt.bfloat16
+I32 = mybir.dt.int32
+U32 = mybir.dt.uint32
+U8 = mybir.dt.uint8
+FP8X4 = mybir.dt.float8_e4m3fn_x4
+FP4X4 = mybir.dt.float4_e2m1fn_x4
+GELU = mybir.ActivationFunctionType.Gelu_apprx_tanh
+
+P = 128
+PACK = 4
+SPAN = P * PACK
+N4 = 4
+N8 = 2
+PASSES = N4 + N8
+W8_ROW = 4
+VEC_COLS = 352
+HALF = T // 2
+
+
+def interleave(engine_copy, dst, src, c0, c1):
+    engine_copy(
+        out=dst[:, PACK * c0 : PACK * c1].rearrange("p (c i j) -> p c j i", i=4, j=PACK),
+        in_=src[:, :, c0:c1].rearrange("p j (c i) -> p c j i", i=4),
+    )
+
+
+def tile_mix_outl_fm_pl_gelu_kernel(
+    tc, x, w8_words, w8_scales, w4_words, w4_scales, b, out_0, out_1, out_2
+):
+    nc = tc.nc
+    with ExitStack() as ctx:
+        keep = ctx.enter_context(tc.tile_pool(name="keep", bufs=1))
+        psum = ctx.enter_context(tc.psum_pool(name="psum", bufs=1))
+        ctx.enter_context(tc.manual_schedule())
+
+        def sb(name, shape, dtype):
+            return keep.tile(shape, dtype, name=name, align_bytes=64)
+
+        x_raw = [sb("x_raw%d" % s, [P, PACK, T], F32) for s in range(PASSES)]
+        x_bf = [sb("x_bf%d" % s, [P, PACK * T], BF16) for s in range(PASSES)]
+        x_codes = [sb("x_codes%d" % s, [P, T], U32) for s in range(PASSES)]
+        x_scales = [sb("x_scales%d" % s, [P, T], U8) for s in range(PASSES)]
+        w4_raw = [sb("w4_raw%d" % h, [P, 2, 4 * SPAN], U8) for h in range(2)]
+        w4_raw_late = sb("w4_raw_late", [P, N4, 2 * SPAN], U8)
+        w8_raw1 = [sb("w8_raw1_%d" % a, [P, SPAN], I32) for a in range(2)]
+        w8_raw0 = sb("w8_raw_first", [P, 2 * SPAN], I32)
+        w8_raw_late = sb("w8_raw_late", [P, N8, SPAN], I32)
+        w4_dealt = [sb("w4_dealt%d" % g, [P, 3, 2 * SPAN], U8) for g in range(N4)]
+        w8_dealt = [sb("w8_dealt%d" % j, [P, 3, SPAN], I32) for j in range(N8)]
+        s_raw = sb("s_raw", [P, N4, M], U8)
+        s_dealt = sb("s_dealt", [P, N4, M], U8)
+        bias = sb("bias", [P, 3, PACK], F32)
+        y = [sb("y%d" % a, [P, PACK, T], F32) for a in range(3)]
+        y_bf = [sb("y_bf%d" % a, [P, PACK * T], BF16) for a in range(3)]
+        y_codes = [sb("y_codes%d" % a, [P, T], U32) for a in range(3)]
+        y_scales01 = sb("y_scales01", [P, 2, T], U8)
+        y_scales2 = sb("y_scales2", [P, T], U8)
+
+        w4_hbm = w4_words.bitcast(I32).rearrange("g p n -> p g n")
+        w8_hbm = w8_words.rearrange("g p n t -> p g (n t)").bitcast(I32)
+        out0_hbm = out_0.rearrange("(a p r) t -> a p r t", p=P, r=PACK)
+        out1_hbm = out_1.rearrange("a p t i -> a p (t i)").bitcast(I32)
+        out2_hbm = out_2.bitcast(I32)
+
+        def load_x(s):
+            k0 = O + SPAN * s if s < N4 else SPAN * (s - N4)
+            nc.sync.dma_start(out=x_raw[s][:], in_=x[k0 : k0 + SPAN, :].rearrange("(p j) t -> p j t", j=PACK))
+
+        def load_w4(h):
+            nc.sync.dma_start(out=w4_raw[h][:].bitcast(I32), in_=w4_hbm[:, 2 * h : 2 * h + 2, 0:SPAN])
+
+        def load_scales():
+            for r in range(4):
+                nc.sync.dma_start(
+                    out=s_raw[r:P:32, :, :].bitcast(I32),
+                    in_=w4_scales.bitcast(I32)[:, r:16:4, :].rearrange("g q n -> q g n"),
+                )
+            for r in range(4):
+                nc.sync.dma_start(
+                    out=s_raw[W8_ROW + r : P : 32, 2:4, :].bitcast(I32),
+                    in_=w8_scales.bitcast(I32)[:, r:16:4, :].rearrange("g q n -> q g n"),
+                )
+
+        def deal_w4(src, g, a0, a1):
+            nc.vector.tensor_copy(
+                out=w4_dealt[g][:, a0:a1, :].rearrange("p a (r m b) -> p a r m b", r=PACK, b=2),
+                in_=src.rearrange("p (a m r b) -> p a r m b", m=P, r=PACK, b=2),
+            )
+
+        def deal_w8(src, j, a0, a1):
+            nc.vector.tensor_copy(
+                out=w8_dealt[j][:, a0:a1, :].rearrange("p a (r c i) -> p a c r i", r=PACK, i=4),
+                in_=src.rearrange("p (a c i r) -> p a c r i", c=P // 4, i=4, r=PACK),
+            )
+
+        def deal_scales(g0, g1):
+            nc.vector.tensor_copy(
+                out=s_dealt[:, g0:g1, :].rearrange("p g (a r m) -> p (g a) r m", r=PACK, m=P),
+                in_=s_raw[:, g0:g1, :].rearrange("p g (a m r) -> p (g a) r m", r=PACK, m=P),
+            )
+
+        def cast_x(s, vec_cols):
+            if vec_cols:
+                interleave(nc.vector.tensor_copy, x_bf[s], x_raw[s], 0, vec_cols)
+            interleave(nc.scalar.copy, x_bf[s], x_raw[s], vec_cols, T)
+
+        def quant_x(s):
+            nc.vector.quantize_mx(out=x_codes[s][:].bitcast(FP8X4), scales=x_scales[s][:], in_=x_bf[s][:])
+
+        acc = {}
+
+        def open_acc(a, r):
+            acc[a, r] = psum.tile([P, T], F32, name="acc%d_%d" % (a, r), tag="bank%d" % ((PACK * a + r) % 8))
+
+        def mm(s, a, r):
+            c0 = SPAN * a + P * r
+            if s < N4:
+                lhs = w4_dealt[s][:, a, 2 * P * r : 2 * P * (r + 1)].bitcast(FP4X4)
+                lhs_scale = s_dealt[:, s, c0 : c0 + P]
+            else:
+                lhs = w8_dealt[s - N4][:, a, P * r : P * (r + 1)].bitcast(FP8X4)
+                lhs_scale = s_dealt[W8_ROW:P, s - 2, c0 : c0 + P]
+            nc.tensor.matmul_mx(
+                out=acc[a, r][:],
+                lhsT=lhs,
+                lhsT_scale=lhs_scale,
+                rhs=x_codes[s][:].bitcast(FP8X4),
+                rhs_scale=x_scales[s][:],
+                start=(s == 0),
+                stop=(s == PASSES - 1),
+            )
+
+        def mm_pass(s, groups):
+            for a in groups:
+                for r in range(PACK):
+                    mm(s, a, r)
+
+        def gelu(a, r, c0=0, c1=T):
+            nc.scalar.activation(
+                out=y[a][:, r, c0:c1], in_=acc[a, r][:, c0:c1], func=GELU, bias=bias[:, a, r : r + 1]
+            )
+
+        def store_y(a, r0, r1):
+            nc.sync.dma_start(out=out0_hbm[a, :, r0:r1, :], in_=y[a][:, r0:r1, :])
+
+        def quant_y(a, plane, c0, c1):
+            nc.vector.quantize_mx(
+                out=y_codes[a][:, c0:c1].bitcast(FP8X4), scales=plane[:, c0:c1], in_=y_bf[a][:, PACK * c0 : PACK * c1]
+            )
+
+        def store_codes(a, c0, c1):
+            nc.sync.dma_start(out=out1_hbm[a, :, c0:c1], in_=y_codes[a][:, c0:c1].bitcast(I32))
+
+        nc.vector.memset(s_raw[:].bitcast(I32), 0)
+        nc.scalar.dma_start(out=bias[:], in_=b.rearrange("(a p r) -> p a r", p=P, r=PACK))
+        load_w4(0)
+        load_scales()
+        load_x(0)
+        load_x(1)
+        load_w4(1)
+        load_x(2)
+        nc.sync.dma_start(out=w8_raw0[:], in_=w8_hbm[:, 0, 0 : 2 * SPAN])
+        load_x(3)
+        load_x(4)
+        load_x(5)
+        for a in range(2):
+            nc.sync.dma_start(out=w8_raw1[a][:], in_=w8_hbm[:, 1, a * SPAN : (a + 1) * SPAN])
+        nc.sync.dma_start(out=w4_raw_late[:].bitcast(I32), in_=w4_hbm[:, :, SPAN : SPAN + SPAN // 2])
+        nc.sync.dma_start(out=w8_raw_late[:], in_=w8_hbm[:, :, 2 * SPAN : 3 * SPAN])
+
+        for a in range(2):
+            for r in range(PACK):
+                open_acc(a, r)
+
+        deal_w4(w4_raw[0][:, 0, :], 0, 0, 2)
+        deal_w4(w4_raw[0][:, 1, :], 1, 0, 2)
+        deal_scales(0, 2)
+        cast_x(0, 0)
+        cast_x(1, 0)
+        quant_x(0)
+        mm_pass(0, (0, 1))
+        deal_scales(2, 4)
+        deal_w4(w4_raw[1][:, 0, :], 2, 0, 2)
+        quant_x(1)
+        mm_pass(1, (0, 1))
+        deal_w4(w4_raw[1][:, 1, :], 3, 0, 2)
+        cast_x(2, VEC_COLS)
+        deal_w8(w8_raw0[:], 0, 0, 2)
+        quant_x(2)
+        mm_pass(2, (0, 1))
+        for s in (3, 4):
+            cast_x(s, VEC_COLS)
+            quant_x(s)
+            mm_pass(s, (0, 1))
+        cast_x(5, VEC_COLS)
+        deal_w8(w8_raw1[0][:], 1, 0, 1)
+        quant_x(5)
+        mm_pass(5, (0,))
+        deal_w8(w8_raw1[1][:], 1, 1, 2)
+        mm_pass(5, (1,))
+        for r in range(PACK):
+            gelu(0, r)
+            if r % 2:
+                store_y(0, r - 1, r + 1)
+            open_acc(2, r)
+        for g in range(N4):
+            deal_w4(w4_raw_late[:, g, :], g, 2, 3)
+        for j in range(N8):
+            deal_w8(w8_raw_late[:, j, :], j, 2, 3)
+        for s in range(3):
+            mm_pass(s, (2,))
+        for r in range(PACK):
+            gelu(1, r)
+            if r % 2:
+                store_y(1, r - 1, r + 1)
+        interleave(nc.vector.tensor_copy, y_bf[0], y[0], 0, T)
+        quant_y(0, y_scales01[:, 0, :], 0, T)
+        store_codes(0, 0, T)
+        interleave(nc.vector.tensor_copy, y_bf[1], y[1], 0, T)
+        quant_y(1, y_scales01[:, 1, :], 0, T)
+        for r in range(PACK):
+            for s in range(3, PASSES):
+                mm(s, 2, r)
+            if r < PACK - 1:
+                gelu(2, r)
+                store_y(2, r, r + 1)
+            if r == 0:
+                store_codes(1, 0, T)
+                for q in range(4):
+                    nc.sync.dma_start(
+                        out=out2_hbm[0:2, 4 * q : 4 * q + 4, :].rearrange("a r w -> r a w"),
+                        in_=y_scales01[32 * q : 32 * q + 4, :, :].bitcast(I32),
+                    )
+        gelu(2, 3, 0, HALF)
+        gelu(2, 3, HALF, T)
+        store_y(2, 3, 4)
+        interleave(nc.vector.tensor_copy, y_bf[2], y[2], 0, HALF)
+        interleave(nc.scalar.copy, y_bf[2], y[2], 384, T)
+        interleave(nc.vector.tensor_copy, y_bf[2], y[2], HALF, 384)
+        quant_y(2, y_scales2, 0, HALF)
+        store_codes(2, 0, HALF)
+        quant_y(2, y_scales2, HALF, T)
+        store_codes(2, HALF, T)
+        for q in range(4):
+            eng = nc.scalar if q % 2 else nc.sync
+            eng.dma_start(out=out2_hbm[2, 4 * q : 4 * q + 4, :], in_=y_scales2[32 * q : 32 * q + 4, :].bitcast(I32))

@@ -21,7 +21,6 @@ N4 = 4
 N8 = 2
 PASSES = N4 + N8
 W8_ROW = 4
-VEC_COLS = 352
 HALF = T // 2
 
 
@@ -70,19 +69,23 @@ def tile_mix_outl_fm_pl_gelu_kernel(
         out1_hbm = out_1.rearrange("a p t i -> a p (t i)").bitcast(I32)
         out2_hbm = out_2.bitcast(I32)
 
-        def load_x(s):
+        def load_x(s, c0=0, c1=T):
             k0 = O + SPAN * s if s < N4 else SPAN * (s - N4)
-            nc.sync.dma_start(out=x_raw[s][:], in_=x[k0 : k0 + SPAN, :].rearrange("(p j) t -> p j t", j=PACK))
+            nc.sync.dma_start(
+                out=x_raw[s][:, :, c0:c1], in_=x[k0 : k0 + SPAN, c0:c1].rearrange("(p j) t -> p j t", j=PACK)
+            )
 
         def load_w4(h):
             nc.sync.dma_start(out=w4_raw[h][:].bitcast(I32), in_=w4_hbm[:, 2 * h : 2 * h + 2, 0:SPAN])
 
-        def load_scales():
+        def load_w4_scales():
             for r in range(4):
-                nc.sync.dma_start(
+                nc.gpsimd.dma_start(
                     out=s_raw[r:P:32, :, :].bitcast(I32),
                     in_=w4_scales.bitcast(I32)[:, r:16:4, :].rearrange("g q n -> q g n"),
                 )
+
+        def load_w8_scales():
             for r in range(4):
                 nc.sync.dma_start(
                     out=s_raw[W8_ROW + r : P : 32, 2:4, :].bitcast(I32),
@@ -101,26 +104,31 @@ def tile_mix_outl_fm_pl_gelu_kernel(
                 in_=src.rearrange("p (a c i r) -> p a c r i", c=P // 4, i=4, r=PACK),
             )
 
-        def deal_scales(g0, g1):
+        def deal_scales(g0, g1, a0, a1):
+            cols = slice(SPAN * a0, SPAN * a1)
             nc.vector.tensor_copy(
-                out=s_dealt[:, g0:g1, :].rearrange("p g (a r m) -> p (g a) r m", r=PACK, m=P),
-                in_=s_raw[:, g0:g1, :].rearrange("p g (a m r) -> p (g a) r m", r=PACK, m=P),
+                out=s_dealt[:, g0:g1, cols].rearrange("p g (a r m) -> p g a r m", r=PACK, m=P),
+                in_=s_raw[:, g0:g1, cols].rearrange("p g (a m r) -> p g a r m", r=PACK, m=P),
             )
 
-        def cast_x(s, vec_cols):
+        def cast_x(s, vec_cols, c0=0, c1=T):
             if vec_cols:
-                interleave(nc.vector.tensor_copy, x_bf[s], x_raw[s], 0, vec_cols)
-            interleave(nc.scalar.copy, x_bf[s], x_raw[s], vec_cols, T)
+                interleave(nc.vector.tensor_copy, x_bf[s], x_raw[s], c0, c0 + vec_cols)
+            interleave(nc.scalar.copy, x_bf[s], x_raw[s], c0 + vec_cols, c1)
 
-        def quant_x(s):
-            nc.vector.quantize_mx(out=x_codes[s][:].bitcast(FP8X4), scales=x_scales[s][:], in_=x_bf[s][:])
+        def quant_x(s, c0=0, c1=T):
+            nc.vector.quantize_mx(
+                out=x_codes[s][:, c0:c1].bitcast(FP8X4),
+                scales=x_scales[s][:, c0:c1],
+                in_=x_bf[s][:, PACK * c0 : PACK * c1],
+            )
 
         acc = {}
 
         def open_acc(a, r):
             acc[a, r] = psum.tile([P, T], F32, name="acc%d_%d" % (a, r), tag="bank%d" % ((PACK * a + r) % 8))
 
-        def mm(s, a, r):
+        def mm(s, a, r, dst=None, t0=0, t1=T):
             c0 = SPAN * a + P * r
             if s < N4:
                 lhs = w4_dealt[s][:, a, 2 * P * r : 2 * P * (r + 1)].bitcast(FP4X4)
@@ -129,11 +137,11 @@ def tile_mix_outl_fm_pl_gelu_kernel(
                 lhs = w8_dealt[s - N4][:, a, P * r : P * (r + 1)].bitcast(FP8X4)
                 lhs_scale = s_dealt[W8_ROW:P, s - 2, c0 : c0 + P]
             nc.tensor.matmul_mx(
-                out=acc[a, r][:],
+                out=acc[a, r][:] if dst is None else dst,
                 lhsT=lhs,
                 lhsT_scale=lhs_scale,
-                rhs=x_codes[s][:].bitcast(FP8X4),
-                rhs_scale=x_scales[s][:],
+                rhs=x_codes[s][:, t0:t1].bitcast(FP8X4),
+                rhs_scale=x_scales[s][:, t0:t1],
                 start=(s == 0),
                 stop=(s == PASSES - 1),
             )
@@ -161,16 +169,18 @@ def tile_mix_outl_fm_pl_gelu_kernel(
 
         nc.vector.memset(s_raw[:].bitcast(I32), 0)
         nc.scalar.dma_start(out=bias[:], in_=b.rearrange("(a p r) -> p a r", p=P, r=PACK))
+        load_w4_scales()
         load_w4(0)
-        load_scales()
         load_x(0)
+        load_w8_scales()
         load_x(1)
         load_w4(1)
         load_x(2)
-        nc.sync.dma_start(out=w8_raw0[:], in_=w8_hbm[:, 0, 0 : 2 * SPAN])
         load_x(3)
         load_x(4)
-        load_x(5)
+        nc.sync.dma_start(out=w8_raw0[:], in_=w8_hbm[:, 0, 0 : 2 * SPAN])
+        load_x(5, 0, HALF)
+        load_x(5, HALF, T)
         for a in range(2):
             nc.sync.dma_start(out=w8_raw1[a][:], in_=w8_hbm[:, 1, a * SPAN : (a + 1) * SPAN])
         nc.sync.dma_start(out=w4_raw_late[:].bitcast(I32), in_=w4_hbm[:, :, SPAN : SPAN + SPAN // 2])
@@ -182,72 +192,85 @@ def tile_mix_outl_fm_pl_gelu_kernel(
 
         deal_w4(w4_raw[0][:, 0, :], 0, 0, 2)
         deal_w4(w4_raw[0][:, 1, :], 1, 0, 2)
-        deal_scales(0, 2)
-        cast_x(0, 0)
-        cast_x(1, 0)
+        cast_x(0, 256)
+        deal_scales(0, 1, 0, 2)
         quant_x(0)
         mm_pass(0, (0, 1))
-        deal_scales(2, 4)
+        deal_scales(1, 4, 0, 2)
+        cast_x(1, 0)
         deal_w4(w4_raw[1][:, 0, :], 2, 0, 2)
         quant_x(1)
         mm_pass(1, (0, 1))
         deal_w4(w4_raw[1][:, 1, :], 3, 0, 2)
-        cast_x(2, VEC_COLS)
-        deal_w8(w8_raw0[:], 0, 0, 2)
+        cast_x(2, 256)
+        deal_scales(0, 2, 2, 3)
         quant_x(2)
         mm_pass(2, (0, 1))
-        for s in (3, 4):
-            cast_x(s, VEC_COLS)
-            quant_x(s)
-            mm_pass(s, (0, 1))
-        cast_x(5, VEC_COLS)
+        cast_x(3, 256)
+        deal_scales(2, 4, 2, 3)
+        quant_x(3)
+        mm_pass(3, (0, 1))
+        cast_x(4, 256)
+        deal_w8(w8_raw0[:], 0, 0, 2)
+        quant_x(4)
+        mm_pass(4, (0, 1))
+        cast_x(5, 160, 0, HALF)
+        quant_x(5, 0, HALF)
+        cast_x(5, 176, HALF, T)
         deal_w8(w8_raw1[0][:], 1, 0, 1)
-        quant_x(5)
+        quant_x(5, HALF, T)
         mm_pass(5, (0,))
         deal_w8(w8_raw1[1][:], 1, 1, 2)
         mm_pass(5, (1,))
         for r in range(PACK):
             gelu(0, r)
-            if r % 2:
-                store_y(0, r - 1, r + 1)
-            open_acc(2, r)
+            if r != 2:
+                store_y(0, min(r, 2), r + 1)
+            if r < PACK - 1:
+                open_acc(2, r)
         for g in range(N4):
             deal_w4(w4_raw_late[:, g, :], g, 2, 3)
         for j in range(N8):
             deal_w8(w8_raw_late[:, j, :], j, 2, 3)
         for s in range(3):
-            mm_pass(s, (2,))
+            for r in range(PACK - 1):
+                mm(s, 2, r)
+        last = []
         for r in range(PACK):
             gelu(1, r)
             if r % 2:
                 store_y(1, r - 1, r + 1)
+            quarter = psum.tile([P, P], F32, name="last%d" % r, tag="bank%d" % (PACK + r))
+            last.append(quarter)
         interleave(nc.vector.tensor_copy, y_bf[0], y[0], 0, T)
         quant_y(0, y_scales01[:, 0, :], 0, T)
         store_codes(0, 0, T)
         interleave(nc.vector.tensor_copy, y_bf[1], y[1], 0, T)
         quant_y(1, y_scales01[:, 1, :], 0, T)
-        for r in range(PACK):
+        for r in range(PACK - 1):
             for s in range(3, PASSES):
                 mm(s, 2, r)
-            if r < PACK - 1:
-                gelu(2, r)
-                store_y(2, r, r + 1)
-            if r == 0:
+            gelu(2, r)
+            store_y(2, r, r + 1)
+            if r == 1:
                 store_codes(1, 0, T)
+            if r == 2:
                 for q in range(4):
                     nc.sync.dma_start(
                         out=out2_hbm[0:2, 4 * q : 4 * q + 4, :].rearrange("a r w -> r a w"),
                         in_=y_scales01[32 * q : 32 * q + 4, :, :].bitcast(I32),
                     )
-        gelu(2, 3, 0, HALF)
-        gelu(2, 3, HALF, T)
+        for u in range(4):
+            for s in range(PASSES):
+                mm(s, 2, 3, last[u][:], P * u, P * (u + 1))
+            nc.scalar.activation(out=y[2][:, 3, P * u : P * (u + 1)], in_=last[u][:], func=GELU, bias=bias[:, 2, 3:4])
+            interleave(nc.vector.tensor_copy, y_bf[2], y[2], P * u, P * (u + 1))
+            if u:
+                quant_y(2, y_scales2, P * (u - 1), P * u)
+            if u == 2:
+                store_codes(2, 0, HALF)
         store_y(2, 3, 4)
-        interleave(nc.vector.tensor_copy, y_bf[2], y[2], 0, HALF)
-        interleave(nc.scalar.copy, y_bf[2], y[2], 384, T)
-        interleave(nc.vector.tensor_copy, y_bf[2], y[2], HALF, 384)
-        quant_y(2, y_scales2, 0, HALF)
-        store_codes(2, 0, HALF)
-        quant_y(2, y_scales2, HALF, T)
+        quant_y(2, y_scales2, 3 * P, T)
         store_codes(2, HALF, T)
         for q in range(4):
             eng = nc.scalar if q % 2 else nc.sync

@@ -80,7 +80,7 @@ def tile_mix_outl_fm_pl_gelu_kernel(
 
         def load_w4_scales():
             for r in range(4):
-                nc.gpsimd.dma_start(
+                nc.sync.dma_start(
                     out=s_raw[r:P:32, :, :].bitcast(I32),
                     in_=w4_scales.bitcast(I32)[:, r:16:4, :].rearrange("g q n -> q g n"),
                 )
@@ -169,13 +169,13 @@ def tile_mix_outl_fm_pl_gelu_kernel(
 
         nc.vector.memset(s_raw[:].bitcast(I32), 0)
         nc.scalar.dma_start(out=bias[:], in_=b.rearrange("(a p r) -> p a r", p=P, r=PACK))
-        load_w4_scales()
         load_w4(0)
         load_x(0)
+        load_w4_scales()
         load_w8_scales()
         load_x(1)
-        load_w4(1)
         load_x(2)
+        load_w4(1)
         load_x(3)
         load_x(4)
         nc.sync.dma_start(out=w8_raw0[:], in_=w8_hbm[:, 0, 0 : 2 * SPAN])
@@ -192,25 +192,24 @@ def tile_mix_outl_fm_pl_gelu_kernel(
 
         deal_w4(w4_raw[0][:, 0, :], 0, 0, 2)
         deal_w4(w4_raw[0][:, 1, :], 1, 0, 2)
-        cast_x(0, 256)
-        deal_scales(0, 1, 0, 2)
+        cast_x(0, 0)
+        deal_scales(0, 2, 0, 2)
+        deal_scales(2, 4, 0, 2)
         quant_x(0)
         mm_pass(0, (0, 1))
-        deal_scales(1, 4, 0, 2)
+        deal_scales(0, 4, 2, 3)
         cast_x(1, 0)
-        deal_w4(w4_raw[1][:, 0, :], 2, 0, 2)
         quant_x(1)
         mm_pass(1, (0, 1))
-        deal_w4(w4_raw[1][:, 1, :], 3, 0, 2)
-        cast_x(2, 256)
-        deal_scales(0, 2, 2, 3)
+        cast_x(2, 0)
+        deal_w4(w4_raw[1][:, 0, :], 2, 0, 2)
         quant_x(2)
         mm_pass(2, (0, 1))
-        cast_x(3, 256)
-        deal_scales(2, 4, 2, 3)
+        cast_x(3, 128)
+        deal_w4(w4_raw[1][:, 1, :], 3, 0, 2)
         quant_x(3)
         mm_pass(3, (0, 1))
-        cast_x(4, 256)
+        cast_x(4, 128)
         deal_w8(w8_raw0[:], 0, 0, 2)
         quant_x(4)
         mm_pass(4, (0, 1))

@@ -57,6 +57,7 @@ def tile_mix_outl_fm_pl_gelu_kernel(
         s_raw = sb("s_raw", [P, N4, M], U8)
         s_dealt = sb("s_dealt", [P, N4, M], U8)
         bias = sb("bias", [P, 3, PACK], F32)
+        warm = sb("warm", [P, 2], F32)
         y = [sb("y%d" % a, [P, PACK, T], F32) for a in range(3)]
         y_bf = [sb("y_bf%d" % a, [P, PACK * T], BF16) for a in range(3)]
         y_codes = [sb("y_codes%d" % a, [P, T], U32) for a in range(3)]
@@ -78,11 +79,11 @@ def tile_mix_outl_fm_pl_gelu_kernel(
         def load_w4(h):
             nc.sync.dma_start(out=w4_raw[h][:].bitcast(I32), in_=w4_hbm[:, 2 * h : 2 * h + 2, 0:SPAN])
 
-        def load_w4_scales():
+        def load_w4_scales(a0, a1):
             for r in range(4):
                 nc.sync.dma_start(
-                    out=s_raw[r:P:32, :, :].bitcast(I32),
-                    in_=w4_scales.bitcast(I32)[:, r:16:4, :].rearrange("g q n -> q g n"),
+                    out=s_raw[r:P:32, :, SPAN * a0 : SPAN * a1].bitcast(I32),
+                    in_=w4_scales.bitcast(I32)[:, r:16:4, P * a0 : P * a1].rearrange("g q n -> q g n"),
                 )
 
         def load_w8_scales():
@@ -169,9 +170,11 @@ def tile_mix_outl_fm_pl_gelu_kernel(
 
         nc.vector.memset(s_raw[:].bitcast(I32), 0)
         nc.scalar.dma_start(out=bias[:], in_=b.rearrange("(a p r) -> p a r", p=P, r=PACK))
+        nc.vector.memset(warm[:, 0:1], 0.0)
+        nc.scalar.activation(out=warm[:, 1:2], in_=warm[:, 0:1], func=GELU)
         load_w4(0)
         load_x(0)
-        load_w4_scales()
+        load_w4_scales(0, 2)
         load_w8_scales()
         load_x(1)
         load_x(2)
@@ -183,7 +186,11 @@ def tile_mix_outl_fm_pl_gelu_kernel(
         load_x(5, HALF, T)
         for a in range(2):
             nc.sync.dma_start(out=w8_raw1[a][:], in_=w8_hbm[:, 1, a * SPAN : (a + 1) * SPAN])
-        nc.sync.dma_start(out=w4_raw_late[:].bitcast(I32), in_=w4_hbm[:, :, SPAN : SPAN + SPAN // 2])
+        load_w4_scales(2, 3)
+        for g in (0, 2):
+            nc.sync.dma_start(
+                out=w4_raw_late[:, g : g + 2, :].bitcast(I32), in_=w4_hbm[:, g : g + 2, SPAN : SPAN + SPAN // 2]
+            )
         nc.sync.dma_start(out=w8_raw_late[:], in_=w8_hbm[:, :, 2 * SPAN : 3 * SPAN])
 
         for a in range(2):
@@ -193,11 +200,10 @@ def tile_mix_outl_fm_pl_gelu_kernel(
         deal_w4(w4_raw[0][:, 0, :], 0, 0, 2)
         deal_w4(w4_raw[0][:, 1, :], 1, 0, 2)
         cast_x(0, 0)
-        deal_scales(0, 2, 0, 2)
-        deal_scales(2, 4, 0, 2)
+        deal_scales(0, 1, 0, 2)
         quant_x(0)
         mm_pass(0, (0, 1))
-        deal_scales(0, 4, 2, 3)
+        deal_scales(1, 4, 0, 2)
         cast_x(1, 0)
         quant_x(1)
         mm_pass(1, (0, 1))
@@ -205,11 +211,11 @@ def tile_mix_outl_fm_pl_gelu_kernel(
         deal_w4(w4_raw[1][:, 0, :], 2, 0, 2)
         quant_x(2)
         mm_pass(2, (0, 1))
-        cast_x(3, 128)
+        cast_x(3, 192)
         deal_w4(w4_raw[1][:, 1, :], 3, 0, 2)
         quant_x(3)
         mm_pass(3, (0, 1))
-        cast_x(4, 128)
+        cast_x(4, 192)
         deal_w8(w8_raw0[:], 0, 0, 2)
         quant_x(4)
         mm_pass(4, (0, 1))
@@ -223,10 +229,10 @@ def tile_mix_outl_fm_pl_gelu_kernel(
         mm_pass(5, (1,))
         for r in range(PACK):
             gelu(0, r)
-            if r != 2:
-                store_y(0, min(r, 2), r + 1)
+            store_y(0, r, r + 1)
             if r < PACK - 1:
                 open_acc(2, r)
+        deal_scales(0, 4, 2, 3)
         for g in range(N4):
             deal_w4(w4_raw_late[:, g, :], g, 2, 3)
         for j in range(N8):
@@ -237,14 +243,14 @@ def tile_mix_outl_fm_pl_gelu_kernel(
         last = []
         for r in range(PACK):
             gelu(1, r)
-            if r % 2:
-                store_y(1, r - 1, r + 1)
+            store_y(1, r, r + 1)
             quarter = psum.tile([P, P], F32, name="last%d" % r, tag="bank%d" % (PACK + r))
             last.append(quarter)
         interleave(nc.vector.tensor_copy, y_bf[0], y[0], 0, T)
         quant_y(0, y_scales01[:, 0, :], 0, T)
         store_codes(0, 0, T)
-        interleave(nc.vector.tensor_copy, y_bf[1], y[1], 0, T)
+        interleave(nc.scalar.copy, y_bf[1], y[1], 256, T)
+        interleave(nc.vector.tensor_copy, y_bf[1], y[1], 0, 256)
         quant_y(1, y_scales01[:, 1, :], 0, T)
         for r in range(PACK - 1):
             for s in range(3, PASSES):
@@ -253,7 +259,6 @@ def tile_mix_outl_fm_pl_gelu_kernel(
             store_y(2, r, r + 1)
             if r == 1:
                 store_codes(1, 0, T)
-            if r == 2:
                 for q in range(4):
                     nc.sync.dma_start(
                         out=out2_hbm[0:2, 4 * q : 4 * q + 4, :].rearrange("a r w -> r a w"),

@@ -88,7 +88,7 @@ def tile_mix_outl_fm_pl_gelu_kernel(
 
         def load_w8_scales():
             for r in range(4):
-                nc.sync.dma_start(
+                nc.gpsimd.dma_start(
                     out=s_raw[W8_ROW + r : P : 32, 2:4, :].bitcast(I32),
                     in_=w8_scales.bitcast(I32)[:, r:16:4, :].rearrange("g q n -> q g n"),
                 )
@@ -169,16 +169,16 @@ def tile_mix_outl_fm_pl_gelu_kernel(
             nc.sync.dma_start(out=out1_hbm[a, :, c0:c1], in_=y_codes[a][:, c0:c1].bitcast(I32))
 
         nc.vector.memset(s_raw[:].bitcast(I32), 0)
-        nc.scalar.dma_start(out=bias[:], in_=b.rearrange("(a p r) -> p a r", p=P, r=PACK))
         nc.vector.memset(warm[:, 0:1], 0.0)
         nc.scalar.activation(out=warm[:, 1:2], in_=warm[:, 0:1], func=GELU)
         load_w4(0)
         load_x(0)
         load_w4_scales(0, 2)
+        nc.sync.dma_start(out=bias[:], in_=b.rearrange("(a p r) -> p a r", p=P, r=PACK))
         load_w8_scales()
         load_x(1)
-        load_x(2)
         load_w4(1)
+        load_x(2)
         load_x(3)
         load_x(4)
         nc.sync.dma_start(out=w8_raw0[:], in_=w8_hbm[:, 0, 0 : 2 * SPAN])
@@ -203,12 +203,13 @@ def tile_mix_outl_fm_pl_gelu_kernel(
         deal_scales(0, 1, 0, 2)
         quant_x(0)
         mm_pass(0, (0, 1))
-        deal_scales(1, 4, 0, 2)
+        deal_scales(1, 2, 0, 2)
         cast_x(1, 0)
+        deal_w4(w4_raw[1][:, 0, :], 2, 0, 2)
         quant_x(1)
         mm_pass(1, (0, 1))
-        cast_x(2, 0)
-        deal_w4(w4_raw[1][:, 0, :], 2, 0, 2)
+        cast_x(2, 192)
+        deal_scales(2, 4, 0, 2)
         quant_x(2)
         mm_pass(2, (0, 1))
         cast_x(3, 192)

from contextlib import ExitStack

import concourse.mybir as mybir

O, K, M, T = 1024, 3072, 1536, 512
FLOPS = 2 * K * M * T

F32 = mybir.dt.float32
BF16 = mybir.dt.bfloat16
I32 = mybir.dt.int32
U32 = mybir.dt.uint32
U8 = mybir.dt.uint8
FP8X4 = mybir.dt.float8_e4m3fn_x4
FP4X4 = mybir.dt.float4_e2m1fn_x4
GELU = mybir.ActivationFunctionType.Gelu_apprx_tanh

P = 128
PACK = 4
SPAN = P * PACK
N4 = 4
N8 = 2
PASSES = N4 + N8
W8_ROW = 4
HALF = T // 2


def interleave(engine_copy, dst, src, c0, c1):
    engine_copy(
        out=dst[:, PACK * c0 : PACK * c1].rearrange("p (c i j) -> p c j i", i=4, j=PACK),
        in_=src[:, :, c0:c1].rearrange("p j (c i) -> p c j i", i=4),
    )


def tile_mix_outl_fm_pl_gelu_kernel(
    tc, x, w8_words, w8_scales, w4_words, w4_scales, b, out_0, out_1, out_2
):
    nc = tc.nc
    with ExitStack() as ctx:
        keep = ctx.enter_context(tc.tile_pool(name="keep", bufs=1))
        psum = ctx.enter_context(tc.psum_pool(name="psum", bufs=1))
        ctx.enter_context(tc.manual_schedule())

        def sb(name, shape, dtype):
            return keep.tile(shape, dtype, name=name, align_bytes=64)

        x_raw = [sb("x_raw%d" % s, [P, PACK, T], F32) for s in range(PASSES)]
        x_bf = [sb("x_bf%d" % s, [P, PACK * T], BF16) for s in range(PASSES)]
        x_codes = [sb("x_codes%d" % s, [P, T], U32) for s in range(PASSES)]
        x_scales = [sb("x_scales%d" % s, [P, T], U8) for s in range(PASSES)]
        w4_raw = [sb("w4_raw%d" % h, [P, 2, 4 * SPAN], U8) for h in range(2)]
        w4_raw_late = sb("w4_raw_late", [P, N4, 2 * SPAN], U8)
        w8_raw1 = [sb("w8_raw1_%d" % a, [P, SPAN], I32) for a in range(2)]
        w8_raw0 = sb("w8_raw_first", [P, 2 * SPAN], I32)
        w8_raw_late = sb("w8_raw_late", [P, N8, SPAN], I32)
        w4_dealt = [sb("w4_dealt%d" % g, [P, 3, 2 * SPAN], U8) for g in range(N4)]
        w8_dealt = [sb("w8_dealt%d" % j, [P, 3, SPAN], I32) for j in range(N8)]
        s_raw = sb("s_raw", [P, N4, M], U8)
        s_dealt = sb("s_dealt", [P, N4, M], U8)
        bias = sb("bias", [P, 3, PACK], F32)
        warm = sb("warm", [P, 2], F32)
        y = [sb("y%d" % a, [P, PACK, T], F32) for a in range(3)]
        y_bf = [sb("y_bf%d" % a, [P, PACK * T], BF16) for a in range(3)]
        y_codes = [sb("y_codes%d" % a, [P, T], U32) for a in range(3)]
        y_scales01 = sb("y_scales01", [P, 2, T], U8)
        y_scales2 = sb("y_scales2", [P, T], U8)

        w4_hbm = w4_words.bitcast(I32).rearrange("g p n -> p g n")
        w8_hbm = w8_words.rearrange("g p n t -> p g (n t)").bitcast(I32)
        out0_hbm = out_0.rearrange("(a p r) t -> a p r t", p=P, r=PACK)
        out1_hbm = out_1.rearrange("a p t i -> a p (t i)").bitcast(I32)
        out2_hbm = out_2.bitcast(I32)

        def load_x(s, c0=0, c1=T):
            k0 = O + SPAN * s if s < N4 else SPAN * (s - N4)
            nc.sync.dma_start(
                out=x_raw[s][:, :, c0:c1], in_=x[k0 : k0 + SPAN, c0:c1].rearrange("(p j) t -> p j t", j=PACK)
            )

        def load_w4(h):
            nc.sync.dma_start(out=w4_raw[h][:].bitcast(I32), in_=w4_hbm[:, 2 * h : 2 * h + 2, 0:SPAN])

        def load_w4_scales(a0, a1):
            for r in range(4):
                nc.sync.dma_start(
                    out=s_raw[r:P:32, :, SPAN * a0 : SPAN * a1].bitcast(I32),
                    in_=w4_scales.bitcast(I32)[:, r:16:4, P * a0 : P * a1].rearrange("g q n -> q g n"),
                )

        def load_w8_scales():
            for r in range(4):
                nc.gpsimd.dma_start(
                    out=s_raw[W8_ROW + r : P : 32, 2:4, :].bitcast(I32),
                    in_=w8_scales.bitcast(I32)[:, r:16:4, :].rearrange("g q n -> q g n"),
                )

        def deal_w4(src, g, a0, a1):
            nc.vector.tensor_copy(
                out=w4_dealt[g][:, a0:a1, :].rearrange("p a (r m b) -> p a r m b", r=PACK, b=2),
                in_=src.rearrange("p (a m r b) -> p a r m b", m=P, r=PACK, b=2),
            )

        def deal_w8(src, j, a0, a1):
            nc.vector.tensor_copy(
                out=w8_dealt[j][:, a0:a1, :].rearrange("p a (r c i) -> p a c r i", r=PACK, i=4),
                in_=src.rearrange("p (a c i r) -> p a c r i", c=P // 4, i=4, r=PACK),
            )

        def deal_scales(g0, g1, a0, a1):
            cols = slice(SPAN * a0, SPAN * a1)
            nc.vector.tensor_copy(
                out=s_dealt[:, g0:g1, cols].rearrange("p g (a r m) -> p g a r m", r=PACK, m=P),
                in_=s_raw[:, g0:g1, cols].rearrange("p g (a m r) -> p g a r m", r=PACK, m=P),
            )

        def cast_x(s, vec_cols, c0=0, c1=T):
            if vec_cols:
                interleave(nc.vector.tensor_copy, x_bf[s], x_raw[s], c0, c0 + vec_cols)
            interleave(nc.scalar.copy, x_bf[s], x_raw[s], c0 + vec_cols, c1)

        def quant_x(s, c0=0, c1=T):
            nc.vector.quantize_mx(
                out=x_codes[s][:, c0:c1].bitcast(FP8X4),
                scales=x_scales[s][:, c0:c1],
                in_=x_bf[s][:, PACK * c0 : PACK * c1],
            )

        acc = {}

        def open_acc(a, r):
            acc[a, r] = psum.tile([P, T], F32, name="acc%d_%d" % (a, r), tag="bank%d" % ((PACK * a + r) % 8))

        def mm(s, a, r, dst=None, t0=0, t1=T):
            c0 = SPAN * a + P * r
            if s < N4:
                lhs = w4_dealt[s][:, a, 2 * P * r : 2 * P * (r + 1)].bitcast(FP4X4)
                lhs_scale = s_dealt[:, s, c0 : c0 + P]
            else:
                lhs = w8_dealt[s - N4][:, a, P * r : P * (r + 1)].bitcast(FP8X4)
                lhs_scale = s_dealt[W8_ROW:P, s - 2, c0 : c0 + P]
            nc.tensor.matmul_mx(
                out=acc[a, r][:] if dst is None else dst,
                lhsT=lhs,
                lhsT_scale=lhs_scale,
                rhs=x_codes[s][:, t0:t1].bitcast(FP8X4),
                rhs_scale=x_scales[s][:, t0:t1],
                start=(s == 0),
                stop=(s == PASSES - 1),
            )

        def mm_pass(s, groups):
            for a in groups:
                for r in range(PACK):
                    mm(s, a, r)

        def gelu(a, r, c0=0, c1=T):
            nc.scalar.activation(
                out=y[a][:, r, c0:c1], in_=acc[a, r][:, c0:c1], func=GELU, bias=bias[:, a, r : r + 1]
            )

        def store_y(a, r0, r1):
            nc.sync.dma_start(out=out0_hbm[a, :, r0:r1, :], in_=y[a][:, r0:r1, :])

        def quant_y(a, plane, c0, c1):
            nc.vector.quantize_mx(
                out=y_codes[a][:, c0:c1].bitcast(FP8X4), scales=plane[:, c0:c1], in_=y_bf[a][:, PACK * c0 : PACK * c1]
            )

        def store_codes(a, c0, c1):
            nc.sync.dma_start(out=out1_hbm[a, :, c0:c1], in_=y_codes[a][:, c0:c1].bitcast(I32))

        nc.vector.memset(s_raw[:].bitcast(I32), 0)
        nc.vector.memset(warm[:, 0:1], 0.0)
        nc.scalar.activation(out=warm[:, 1:2], in_=warm[:, 0:1], func=GELU)
        load_w4(0)
        load_x(0)
        load_w4_scales(0, 2)
        nc.sync.dma_start(out=bias[:], in_=b.rearrange("(a p r) -> p a r", p=P, r=PACK))
        load_w8_scales()
        load_x(1)
        load_w4(1)
        load_x(2)
        load_x(3)
        load_x(4)
        nc.sync.dma_start(out=w8_raw0[:], in_=w8_hbm[:, 0, 0 : 2 * SPAN])
        load_x(5, 0, HALF)
        load_x(5, HALF, T)
        for a in range(2):
            nc.sync.dma_start(out=w8_raw1[a][:], in_=w8_hbm[:, 1, a * SPAN : (a + 1) * SPAN])
        load_w4_scales(2, 3)
        for g in (0, 2):
            nc.sync.dma_start(
                out=w4_raw_late[:, g : g + 2, :].bitcast(I32), in_=w4_hbm[:, g : g + 2, SPAN : SPAN + SPAN // 2]
            )
        nc.sync.dma_start(out=w8_raw_late[:], in_=w8_hbm[:, :, 2 * SPAN : 3 * SPAN])

        for a in range(2):
            for r in range(PACK):
                open_acc(a, r)

        deal_w4(w4_raw[0][:, 0, :], 0, 0, 2)
        deal_w4(w4_raw[0][:, 1, :], 1, 0, 2)
        cast_x(0, 0)
        deal_scales(0, 1, 0, 2)
        quant_x(0)
        mm_pass(0, (0, 1))
        deal_scales(1, 2, 0, 2)
        cast_x(1, 0)
        deal_w4(w4_raw[1][:, 0, :], 2, 0, 2)
        quant_x(1)
        mm_pass(1, (0, 1))
        cast_x(2, 192)
        deal_scales(2, 4, 0, 2)
        quant_x(2)
        mm_pass(2, (0, 1))
        cast_x(3, 192)
        deal_w4(w4_raw[1][:, 1, :], 3, 0, 2)
        quant_x(3)
        mm_pass(3, (0, 1))
        cast_x(4, 192)
        deal_w8(w8_raw0[:], 0, 0, 2)
        quant_x(4)
        mm_pass(4, (0, 1))
        cast_x(5, 160, 0, HALF)
        quant_x(5, 0, HALF)
        cast_x(5, 176, HALF, T)
        deal_w8(w8_raw1[0][:], 1, 0, 1)
        quant_x(5, HALF, T)
        mm_pass(5, (0,))
        deal_w8(w8_raw1[1][:], 1, 1, 2)
        mm_pass(5, (1,))
        for r in range(PACK):
            gelu(0, r)
            store_y(0, r, r + 1)
            if r < PACK - 1:
                open_acc(2, r)
        deal_scales(0, 4, 2, 3)
        for g in range(N4):
            deal_w4(w4_raw_late[:, g, :], g, 2, 3)
        for j in range(N8):
            deal_w8(w8_raw_late[:, j, :], j, 2, 3)
        for s in range(3):
            for r in range(PACK - 1):
                mm(s, 2, r)
        last = []
        for r in range(PACK):
            gelu(1, r)
            store_y(1, r, r + 1)
            quarter = psum.tile([P, P], F32, name="last%d" % r, tag="bank%d" % (PACK + r))
            last.append(quarter)
        interleave(nc.vector.tensor_copy, y_bf[0], y[0], 0, T)
        quant_y(0, y_scales01[:, 0, :], 0, T)
        store_codes(0, 0, T)
        interleave(nc.scalar.copy, y_bf[1], y[1], 256, T)
        interleave(nc.vector.tensor_copy, y_bf[1], y[1], 0, 256)
        quant_y(1, y_scales01[:, 1, :], 0, T)
        for r in range(PACK - 1):
            for s in range(3, PASSES):
                mm(s, 2, r)
            gelu(2, r)
            store_y(2, r, r + 1)
            if r == 1:
                store_codes(1, 0, T)
                for q in range(4):
                    nc.sync.dma_start(
                        out=out2_hbm[0:2, 4 * q : 4 * q + 4, :].rearrange("a r w -> r a w"),
                        in_=y_scales01[32 * q : 32 * q + 4, :, :].bitcast(I32),
                    )
        for u in range(4):
            for s in range(PASSES):
                mm(s, 2, 3, last[u][:], P * u, P * (u + 1))
            nc.scalar.activation(out=y[2][:, 3, P * u : P * (u + 1)], in_=last[u][:], func=GELU, bias=bias[:, 2, 3:4])
            interleave(nc.vector.tensor_copy, y_bf[2], y[2], P * u, P * (u + 1))
            if u:
                quant_y(2, y_scales2, P * (u - 1), P * u)
            if u == 2:
                store_codes(2, 0, HALF)
        store_y(2, 3, 4)
        quant_y(2, y_scales2, 3 * P, T)
        store_codes(2, HALF, T)
        for q in range(4):
            eng = nc.scalar if q % 2 else nc.sync
            eng.dma_start(out=out2_hbm[2, 4 * q : 4 * q + 4, :], in_=y_scales2[32 * q : 32 * q + 4, :].bitcast(I32))
